import numpy as np
import ml_dtypes


def mxq(x, axis, fmt="e4m3"):
    dtype, down = {"e4m3": (ml_dtypes.float8_e4m3fn, 7), "e5m2": (ml_dtypes.float8_e5m2, 14)}[fmt]
    v = np.moveaxis(np.asarray(x, np.float32).astype(ml_dtypes.bfloat16).astype(np.float64), axis, -1)
    blocks = v.reshape(v.shape[:-1] + (-1, 32))
    amax = np.abs(blocks).max(-1, keepdims=True)
    byte = np.maximum(np.where(amax > 0, np.frexp(amax)[1] - 1 + 127, 0) - down, 1)
    scale = np.exp2(byte - 127.0)
    codes = (blocks / scale).astype(np.float32).astype(dtype).astype(np.float64)
    return np.moveaxis((codes * scale).reshape(v.shape), -1, axis)


WIDE = False


def mx_kscale(k):
    if not WIDE:
        return np.ones(k)
    levels = np.array([10, -10, 5, -5, 0])
    if k % 512:
        return np.exp2(np.random.permutation(np.resize(levels, k // 32))).repeat(32)
    a = np.empty((k // 512, 16))
    for p in range(k // 512):
        a[p, :8] = np.random.permutation(np.resize(levels, 8))
        for g in range(8):
            far = levels[np.abs(levels - a[p, g]) >= 10]
            a[p, g + 8] = far[np.random.randint(len(far))]
    return np.exp2(a.ravel()).repeat(32)


def f64(x):
    return np.asarray(x).astype(np.float64)


def striped(idx):
    return np.tile(idx.reshape(-1, 16).T, (8, 1)).astype(np.uint16)


def unstriped(offs):
    return offs[:16].T.reshape(-1).astype(np.int64)


def striped8(idx):
    return np.concatenate([x.reshape(-1, 16).T for x in idx]).astype(np.uint16)


def runs(offs, k):
    lists = np.stack([offs[16 * r : 16 * r + 16].T.reshape(-1) for r in range(8)]).astype(np.int64)
    return lists[np.arange(k) % 512 // 64]


def pack_weight(w):
    k, n = w.shape
    w = f64(np.asarray(w, np.float32).astype(ml_dtypes.bfloat16)).reshape(k // 32, 32, n)
    amax = np.abs(w).max(1)
    byte = np.clip(np.where(amax > 0, np.frexp(amax)[1] - 1 + 127 - 7, 1), 1, 254)
    scaled = (w * np.exp2(127.0 - byte)[:, None, :]).reshape(k, n).astype(np.float32)
    words = np.ascontiguousarray(scaled.reshape(k // 512, 128, 4, n).transpose(0, 1, 3, 2)).astype(ml_dtypes.float8_e4m3fn).view(np.uint8)
    return words, np.ascontiguousarray(byte.astype(np.uint8).reshape(k // 512, 16, n))


def unpack_weight(words, scales):
    g, p, n, _ = words.shape
    vals = np.ascontiguousarray(words).view(ml_dtypes.float8_e4m3fn).astype(np.float64) * np.repeat(np.exp2(scales.astype(np.float64) - 127.0), 8, axis=1)[..., None]
    return vals.transpose(0, 1, 3, 2).reshape(g * 512, n)


K, T, S, G, H, W, C = 512, 1024, 512, 2048, 512, 384, 512


def setup_inputs():
    n = np.random.standard_normal
    s = mx_kscale(K)[:, None]
    packed_xT = pack_weight(n((K, T)) * s)
    packed_dT = pack_weight(n((K, G)) / s)
    return {
        "x_words": packed_xT[0],
        "x_scales": packed_xT[1],
        "d_words": packed_dT[0],
        "d_scales": packed_dT[1],
        "gs": (np.random.uniform(0.5, 1.5, (K, 1)) / s).astype(np.float32),
        "tau": np.random.uniform(0.3, 0.9, (H, 1)).astype(np.float32),
        "offs": striped(np.random.permutation(T)[:S]),
        "k1": striped8(np.random.randint(0, G, (8, H))),
        "n1": striped(np.random.permutation(S)[:W]),
        "n2": striped(np.random.permutation(S)[:W]),
        "cand": striped(np.random.permutation(T)[:C]),
        "two": striped(np.random.permutation(T)[:S]),
        "k2": striped8(np.random.randint(0, G, (8, H))),
        "n3": striped8(np.stack([np.random.permutation(S) for _ in range(8)])),
        "n4": striped8(np.stack([np.random.permutation(S) for _ in range(8)])),
    }


def reference(x_words, x_scales, d_words, d_scales, gs, tau, offs, k1, n1, n2, cand, two, k2, n3, n4):
    d_k2 = unpack_weight(d_words, d_scales)[np.arange(K)[:, None], runs(k2, K)]
    x_two = unpack_weight(x_words, x_scales)[:, unstriped(two)]
    b = 0.0625 * (d_k2.T @ x_two)
    top = b.max(axis=1, keepdims=True)
    ea = np.exp(f64(tau) * (b[np.arange(H)[:, None], runs(n3, H)] - top))
    x_cand = unpack_weight(x_words, x_scales)[:, unstriped(cand)]
    d_k1 = unpack_weight(d_words, d_scales)[np.arange(K)[:, None], runs(k1, K)]
    xq = unpack_weight(x_words, x_scales)[:, unstriped(offs)]
    h = 0.0625 * (d_k1.T @ xq)
    pa = h[:, unstriped(n2)]
    old = h[:, unstriped(n1)]
    ra = np.minimum(pa, old) - (0.5 * pa)
    ds = h.copy()
    ds[:, unstriped(n1)] = ra
    z = f64(gs) * ds
    a = 0.0625 * ((x_cand.T @ mxq(z, 0, "e4m3")))
    return (2.0 * ea) * (a - (a[np.arange(C)[:, None], runs(n4, C)])) - (0.5 * b)

@@ -1,0 +1,222 @@
+from contextlib import ExitStack
+
+import concourse.mybir as mybir
+
+K, T, S, G, H, W, C = 512, 1024, 512, 2048, 512, 384, 512
+FLOPS = 3 * 2 * 512 * 512 * 512
+
+F32 = mybir.dt.float32
+BF16 = mybir.dt.bfloat16
+I32 = mybir.dt.int32
+U32 = mybir.dt.uint32
+U16 = mybir.dt.uint16
+U8 = mybir.dt.uint8
+FP8X4 = mybir.dt.float8_e4m3fn_x4
+ALU = mybir.AluOpType
+ACT = mybir.ActivationFunctionType
+
+P = 128
+PACK = 4
+HALF = S // 2
+SCALAR_SCATTER_TILES = (0, 1)
+STAGE_AT = {
+    "words_two": 64,
+    "picked_w_k1": 2048,
+    "scales_two": 2112,
+    "scales_cand": 2624,
+    "picked_b_k2": 3840,
+    "picked_w_k2": 4096,
+    "words_cand": 6080,
+    "scales_offs": 8192,
+    "picked_b_k1": 8448,
+    "words_offs": 8704,
+}
+
+
+def tile_picked_pqcjpxbkmin_none_p_kernel(
+    tc, x_words, x_scales, d_words, d_scales, gs, tau, offs, k1, n1, n2, cand, two, k2, n3, n4, out
+):
+    nc = tc.nc
+    with ExitStack() as ctx:
+        keep = ctx.enter_context(tc.tile_pool(name="keep", bufs=1))
+        psum = ctx.enter_context(tc.psum_pool(name="psum", bufs=1))
+
+        stage = ctx.enter_context(tc.tile_pool(name="stage", bufs=1))
+
+        def tile(name, width, dtype):
+            if name in STAGE_AT:
+                return stage.tile([P, width], dtype, name=name, align_bytes=64, offset=STAGE_AT[name])
+            return keep.tile([P, width], dtype, name=name, align_bytes=64)
+
+        def load_list(name, src):
+            t = keep.tile([P, src.shape[1]], U16, name=name)
+            nc.sync.dma_start(t[:], src)
+            return t
+
+        def zeroed_bytes(name, width, engine):
+            t = tile(name, width, U8)
+            engine.memset(t[:].bitcast(I32), 0)
+            return t
+
+        d_bytes = zeroed_bytes("d_bytes", G, nc.vector)
+        x_bytes = zeroed_bytes("x_bytes", T, nc.vector)
+
+        d_rows = d_scales[0].rearrange("(r e) n -> e r n", e=2)
+        for e in range(2):
+            nc.sync.dma_start(d_bytes[e:P:16, :].bitcast(I32), d_rows[e].bitcast(I32))
+        k1_t = load_list("k1_t", k1)
+        offs_t = load_list("offs_t", offs)
+        k2_t = load_list("k2_t", k2)
+        two_t = load_list("two_t", two)
+        x_tab = tile("x_tab", T, U32)
+        nc.sync.dma_start(x_tab[:].bitcast(I32), x_words[0].rearrange("p n t -> p (n t)").bitcast(I32))
+        for q in range(4):
+            nc.sync.dma_start(x_bytes[32 * q : 32 * q + 4, :].bitcast(I32), x_scales[0, 4 * q : 4 * q + 4, :].bitcast(I32))
+        d_tab = tile("d_tab", G, U32)
+        nc.sync.dma_start(d_tab[:].bitcast(I32), d_words[0].rearrange("p n t -> p (n t)").bitcast(I32))
+        n2_t = load_list("n2_t", n2)
+        n1_t = load_list("n1_t", n1)
+        cand_t = load_list("cand_t", cand)
+        gs_t = tile("gs_t", PACK, F32)
+        nc.sync.dma_start(gs_t[:], gs.rearrange("(p t) o -> p (t o)", t=PACK))
+        tau_t = tile("tau_t", PACK, F32)
+        nc.sync.dma_start(tau_t[:], tau.rearrange("(p t) o -> p (t o)", t=PACK))
+        n3_t = load_list("n3_t", n3)
+        n4_t = load_list("n4_t", n4)
+
+        def code_bytes(name, lst, queue):
+            picked = tile("picked_b_" + name, H, U8)
+            nc.vector.tensor_copy(picked[:], d_bytes[:].indirect(lst[:]))
+            dealt = tile("dealt_b_" + name, H, U8)
+            nc.vector.tensor_copy(
+                dealt[:].rearrange("p (t m) -> p t m", t=PACK), picked[:].rearrange("p (m t) -> p t m", t=PACK)
+            )
+            placed = tile("placed_" + name, H, U8)
+            nc.vector.tensor_copy(placed[:].bitcast(I32), dealt[:].bitcast(I32))
+            for e in range(2):
+                queue.dma_start(placed[2 + e : P : 32, :].bitcast(I32), dealt[16 + e : P : 32, :].bitcast(I32))
+            return placed
+
+        def code_words(name, lst):
+            picked = tile("picked_w_" + name, H, U32)
+            nc.vector.tensor_copy(picked[:], d_tab[:].indirect(lst[:]))
+            dealt = tile("dealt_w_" + name, H, U32)
+            nc.vector.tensor_copy(
+                dealt[:].rearrange("p (t m i) -> p m t i", t=PACK, i=4),
+                picked[:].rearrange("p (m i t) -> p m t i", t=PACK, i=4),
+            )
+            return dealt
+
+        def tokens(name, lst, dealt):
+            words = tile("words_" + name, S, U32)
+            scales = tile("scales_" + name, S, U8)
+            for dst, table in ((words, x_tab), (scales, x_bytes)):
+                view = dst[:].rearrange("p (t m) -> p m t", t=PACK) if dealt else dst[:]
+                nc.vector.tensor_copy(view, table[:].indirect(lst[:]))
+            return words, scales
+
+        def product(bank, t, lhs_w, lhs_s, rhs_w, rhs_s):
+            acc = psum.tile([P, S], F32, name="acc", tag=bank)
+            cols = slice(P * t, P * (t + 1))
+            nc.tensor.matmul_mx(
+                out=acc[:], lhsT=lhs_w[:, cols].bitcast(FP8X4), lhsT_scale=lhs_s[:, cols],
+                rhs=rhs_w[:].bitcast(FP8X4), rhs_scale=rhs_s[:], start=True, stop=True,
+            )
+            return acc
+
+        k1_s = code_bytes("k1", k1_t, nc.scalar)
+        xq_w, xq_s = tokens("offs", offs_t, False)
+        k1_w = code_words("k1", k1_t)
+        h, npa, old = [], [], []
+        for t in range(PACK):
+            acc = product("h%d" % t, t, k1_w, k1_s, xq_w, xq_s)
+            h.append(tile("h%d" % t, S, F32))
+            npa.append(tile("npa%d" % t, W, F32))
+            old.append(tile("old%d" % t, W, F32))
+            nc.scalar.activation(h[t][:], acc[:], ACT.Copy, scale=0.0625)
+            nc.scalar.activation(npa[t][:], h[t][:].indirect(n2_t[:]), ACT.Copy, scale=-0.5)
+            nc.scalar.activation(old[t][:], h[t][:].indirect(n1_t[:]), ACT.Copy)
+
+        k2_s = code_bytes("k2", k2_t, nc.sync)
+        x2_w, x2_s = tokens("two", two_t, False)
+        k2_w = code_words("k2", k2_t)
+        xc_w, xc_s = tokens("cand", cand_t, True)
+
+        pairs = tile("pairs", PACK * S, BF16)
+        pair_view = pairs[:].rearrange("p (u c e) -> p u e c", u=2, e=2)
+
+        def update(t):
+            low = tile("low%d" % t, W, F32)
+            nc.vector.scalar_tensor_tensor(low[:], npa[t][:], -2.0, old[t][:], ALU.mult, ALU.min)
+            if t in SCALAR_SCATTER_TILES:
+                ra = tile("ra%d" % t, W, F32)
+                nc.vector.tensor_tensor(ra[:], low[:], npa[t][:], ALU.add)
+                nc.scalar.activation(h[t][:].indirect(n1_t[:]), ra[:], ACT.Copy)
+            else:
+                for c in range(2):
+                    cols = slice(c * W // 2, (c + 1) * W // 2)
+                    nc.vector.tensor_tensor(
+                        h[t][:].indirect(n1_t[:, c * W // 32 : (c + 1) * W // 32]), low[:, cols], npa[t][:, cols], ALU.add
+                    )
+
+        def weigh(t):
+            nc.vector.tensor_scalar(pair_view[:, t // 2, t % 2, :], h[t][:], gs_t[:, t : t + 1], None, ALU.mult)
+
+        for t in range(3):
+            update(t)
+
+        top = tile("top", PACK, F32)
+        b = []
+        for t in range(PACK):
+            acc = product("b%d" % t, t, k2_w, k2_s, x2_w, x2_s)
+            bt = tile("b%d" % t, S, F32)
+            nc.vector.tensor_scalar(bt[:], acc[:], 0.0625, None, ALU.mult, ALU.max, accum_out=top[:, t : t + 1])
+            b.append(bt)
+        bias = tile("bias", PACK, F32)
+        nc.vector.scalar_tensor_tensor(bias[:], top[:], -1.0, tau_t[:], ALU.mult, ALU.mult)
+
+        update(3)
+        for t in range(PACK):
+            weigh(t)
+
+        z = tile("z", PACK * S, BF16)
+        nc.vector.tensor_copy(
+            z[:].bitcast(I32).rearrange("p (c u) -> p c u", u=2),
+            pairs[:].bitcast(I32).rearrange("p (u c) -> p c u", u=2),
+        )
+        z_w = tile("z_w", S, U32)
+        z_s = tile("z_s", S, U8)
+        nc.vector.quantize_mx(out=z_w[:].bitcast(FP8X4), scales=z_s[:], in_=z[:])
+
+        ea = []
+        for t in range(PACK):
+            e = tile("ea%d" % t, S, F32)
+            for c in range(2):
+                nc.scalar.activation(
+                    e[:, c * HALF : (c + 1) * HALF], b[t][:].indirect(n3_t[:, c * 16 : (c + 1) * 16]), ACT.Exp,
+                    bias=bias[:, t : t + 1], scale=tau_t[:, t : t + 1],
+                )
+            ea.append(e)
+
+        rows = out.rearrange("(p t) n -> t p n", t=PACK)
+        for t in range(PACK):
+            acc = product("h%d" % (t % 2), t, xc_w, xc_s, z_w, z_s)
+            a2 = tile("a2_%d" % t, S, F32)
+            if t == 1:
+                nc.vector.tensor_scalar(a2[:], acc[:], 0.125, None, ALU.mult)
+            else:
+                nc.scalar.activation(a2[:], acc[:], ACT.Copy, scale=0.125)
+            a4 = tile("a4_%d" % t, S, F32)
+            d = tile("d%d" % t, S, F32)
+            m = tile("m%d" % t, S, F32)
+            o = tile("o%d" % t, S, F32)
+            halves = [slice(c * HALF, (c + 1) * HALF) for c in range(2)]
+            for c in range(2):
+                nc.scalar.activation(a4[:, halves[c]], a2[:].indirect(n4_t[:, c * 16 : (c + 1) * 16]), ACT.Copy)
+            for c in halves:
+                nc.vector.tensor_tensor(d[:, c], a2[:, c], a4[:, c], ALU.subtract)
+            for c in halves:
+                nc.vector.tensor_tensor(m[:, c], d[:, c], ea[t][:, c], ALU.mult)
+            for c in halves:
+                nc.vector.scalar_tensor_tensor(o[:, c], b[t][:, c], -0.5, m[:, c], ALU.mult, ALU.add)
+            nc.sync.dma_start(rows[t], o[:])

@@ -18,18 +18,28 @@ ACT = mybir.ActivationFunctionType
 P = 128
 PACK = 4
 HALF = S // 2
-SCALAR_SCATTER_TILES = (0, 1)
+RUN = 4
+SCALAR_SCATTER_TILES = (0, 1, 2)
 STAGE_AT = {
-    "words_two": 64,
-    "picked_w_k1": 2048,
-    "scales_two": 2112,
-    "scales_cand": 2624,
-    "picked_b_k2": 3840,
-    "picked_w_k2": 4096,
-    "words_cand": 6080,
-    "scales_offs": 8192,
-    "picked_b_k1": 8448,
-    "words_offs": 8704,
+    "words_offs0": 0,
+    "scales_two": 0,
+    "picked_b_k2": 768,
+    "picked_w_k2": 1024,
+    "words_cand": 3072,
+    "low0": 4608,
+    "scales_cand": 5120,
+    "low1": 6144,
+    "b0": 6144,
+    "b1": 8192,
+    "low2": 9728,
+    "b2": 10240,
+    "ea0": 12288,
+    "ra2": 13824,
+    "ea1": 14336,
+    "planes": 16384,
+    "b3": 16384,
+    "a4_2": 20480,
+    "ea3": 20480,
 }
 
 
@@ -68,31 +78,41 @@ def tile_picked_pqcjpxbkmin_none_p_kernel(
         offs_t = load_list("offs_t", offs)
         k2_t = load_list("k2_t", k2)
         two_t = load_list("two_t", two)
-        x_tab = tile("x_tab", T, U32)
-        nc.sync.dma_start(x_tab[:].bitcast(I32), x_words[0].rearrange("p n t -> p (n t)").bitcast(I32))
-        for q in range(4):
-            nc.sync.dma_start(x_bytes[32 * q : 32 * q + 4, :].bitcast(I32), x_scales[0, 4 * q : 4 * q + 4, :].bitcast(I32))
         d_tab = tile("d_tab", G, U32)
         nc.sync.dma_start(d_tab[:].bitcast(I32), d_words[0].rearrange("p n t -> p (n t)").bitcast(I32))
+        for q in range(4):
+            nc.sync.dma_start(x_bytes[32 * q : 32 * q + 4, :].bitcast(I32), x_scales[0, 4 * q : 4 * q + 4, :].bitcast(I32))
+        x_tab = tile("x_tab", T, U32)
+        nc.sync.dma_start(x_tab[:].bitcast(I32), x_words[0].rearrange("p n t -> p (n t)").bitcast(I32))
         n2_t = load_list("n2_t", n2)
         n1_t = load_list("n1_t", n1)
         cand_t = load_list("cand_t", cand)
         gs_t = tile("gs_t", PACK, F32)
         nc.sync.dma_start(gs_t[:], gs.rearrange("(p t) o -> p (t o)", t=PACK))
-        tau_t = tile("tau_t", PACK, F32)
-        nc.sync.dma_start(tau_t[:], tau.rearrange("(p t) o -> p (t o)", t=PACK))
+        tau_rows = tau.rearrange("(g t i) o -> t g i o", t=PACK, i=RUN)
+        tau_t = [tile("tau%d" % t, 1, F32) for t in range(PACK)]
         n3_t = load_list("n3_t", n3)
+        for t in range(PACK):
+            with nc.allow_non_contiguous_dma(reason="one rate for each partition"):
+                nc.sync.dma_start(tau_t[t][:], tau_rows[t])
         n4_t = load_list("n4_t", n4)
 
         def code_bytes(name, lst, queue):
             picked = tile("picked_b_" + name, H, U8)
             nc.vector.tensor_copy(picked[:], d_bytes[:].indirect(lst[:]))
             dealt = tile("dealt_b_" + name, H, U8)
-            nc.vector.tensor_copy(
-                dealt[:].rearrange("p (t m) -> p t m", t=PACK), picked[:].rearrange("p (m t) -> p t m", t=PACK)
-            )
             placed = tile("placed_" + name, H, U8)
-            nc.vector.tensor_copy(placed[:].bitcast(I32), dealt[:].bitcast(I32))
+            if name == "k1":
+                nc.vector.tensor_copy(
+                    dealt[:].rearrange("p (t m) -> p t m", t=PACK), picked[:].rearrange("p (m t) -> p t m", t=PACK)
+                )
+                nc.vector.tensor_copy(placed[:].bitcast(I32), dealt[:].bitcast(I32))
+            else:
+                for dst in (dealt, placed):
+                    nc.vector.tensor_copy(
+                        dst[:].bitcast(I32).rearrange("p (t g) -> p t g", t=PACK),
+                        picked[:].bitcast(I32).rearrange("p (g t) -> p t g", t=PACK),
+                    )
             for e in range(2):
                 queue.dma_start(placed[2 + e : P : 32, :].bitcast(I32), dealt[16 + e : P : 32, :].bitcast(I32))
             return placed
@@ -101,49 +121,63 @@ def tile_picked_pqcjpxbkmin_none_p_kernel(
             picked = tile("picked_w_" + name, H, U32)
             nc.vector.tensor_copy(picked[:], d_tab[:].indirect(lst[:]))
             dealt = tile("dealt_w_" + name, H, U32)
-            nc.vector.tensor_copy(
-                dealt[:].rearrange("p (t m i) -> p m t i", t=PACK, i=4),
-                picked[:].rearrange("p (m i t) -> p m t i", t=PACK, i=4),
-            )
+            if name == "k1":
+                nc.vector.tensor_copy(
+                    dealt[:].rearrange("p (t m i) -> p m t i", t=PACK, i=4),
+                    picked[:].rearrange("p (m i t) -> p m t i", t=PACK, i=4),
+                )
+            else:
+                nc.vector.tensor_copy(
+                    dealt[:].rearrange("p (t g i) -> p t g i", t=PACK, i=RUN),
+                    picked[:].rearrange("p (g t i) -> p t g i", t=PACK, i=RUN),
+                )
             return dealt
 
         def tokens(name, lst, dealt):
             words = tile("words_" + name, S, U32)
             scales = tile("scales_" + name, S, U8)
             for dst, table in ((words, x_tab), (scales, x_bytes)):
-                view = dst[:].rearrange("p (t m) -> p m t", t=PACK) if dealt else dst[:]
+                view = dst[:].rearrange("p (t g i) -> p g t i", t=PACK, i=RUN) if dealt else dst[:]
                 nc.vector.tensor_copy(view, table[:].indirect(lst[:]))
             return words, scales
 
-        def product(bank, t, lhs_w, lhs_s, rhs_w, rhs_s):
-            acc = psum.tile([P, S], F32, name="acc", tag=bank)
-            cols = slice(P * t, P * (t + 1))
+        halves = [slice(c * HALF, (c + 1) * HALF) for c in range(2)]
+        whole = slice(0, S)
+
+        def list_half(lst, c):
+            return lst[:, c * HALF // 16 : (c + 1) * HALF // 16]
+
+        def product(bank, t, lhs_w, lhs_s, rhs_w, rhs_s, cols):
+            acc = psum.tile([P, cols.stop - cols.start], F32, name="acc", tag=bank)
+            rows_t = slice(P * t, P * (t + 1))
             nc.tensor.matmul_mx(
-                out=acc[:], lhsT=lhs_w[:, cols].bitcast(FP8X4), lhsT_scale=lhs_s[:, cols],
-                rhs=rhs_w[:].bitcast(FP8X4), rhs_scale=rhs_s[:], start=True, stop=True,
+                out=acc[:], lhsT=lhs_w[:, rows_t].bitcast(FP8X4), lhsT_scale=lhs_s[:, rows_t],
+                rhs=rhs_w[:, cols].bitcast(FP8X4), rhs_scale=rhs_s[:, cols], start=True, stop=True,
             )
             return acc
 
         k1_s = code_bytes("k1", k1_t, nc.scalar)
-        xq_w, xq_s = tokens("offs", offs_t, False)
         k1_w = code_words("k1", k1_t)
-        h, npa, old = [], [], []
+        xq_w = [tile("words_offs%d" % c, HALF, U32) for c in range(2)]
+        xq_s = [tile("scales_offs%d" % c, HALF, U8) for c in range(2)]
+        for c in range(2):
+            nc.vector.tensor_copy(xq_s[c][:], x_bytes[:].indirect(list_half(offs_t, c)))
+            nc.vector.tensor_copy(xq_w[c][:], x_tab[:].indirect(list_half(offs_t, c)))
+        h = [tile("h%d" % t, S, F32) for t in range(PACK)]
+        npa = [tile("npa%d" % t, W, F32) for t in range(PACK)]
+        old = [tile("old%d" % t, W, F32) for t in range(PACK)]
         for t in range(PACK):
-            acc = product("h%d" % t, t, k1_w, k1_s, xq_w, xq_s)
-            h.append(tile("h%d" % t, S, F32))
-            npa.append(tile("npa%d" % t, W, F32))
-            old.append(tile("old%d" % t, W, F32))
-            nc.scalar.activation(h[t][:], acc[:], ACT.Copy, scale=0.0625)
+            acc = product("b%d" % t, t, k1_w, k1_s, xq_w[0], xq_s[0], halves[0])
+            nc.scalar.activation(h[t][:, halves[0]], acc[:], ACT.Copy, scale=0.0625)
+        for t in range(PACK):
+            acc = product("h%d" % t, t, k1_w, k1_s, xq_w[1], xq_s[1], halves[0])
+            nc.scalar.activation(h[t][:, halves[1]], acc[:], ACT.Copy, scale=0.0625)
             nc.scalar.activation(npa[t][:], h[t][:].indirect(n2_t[:]), ACT.Copy, scale=-0.5)
             nc.scalar.activation(old[t][:], h[t][:].indirect(n1_t[:]), ACT.Copy)
 
         k2_s = code_bytes("k2", k2_t, nc.sync)
         x2_w, x2_s = tokens("two", two_t, False)
         k2_w = code_words("k2", k2_t)
-        xc_w, xc_s = tokens("cand", cand_t, True)
-
-        pairs = tile("pairs", PACK * S, BF16)
-        pair_view = pairs[:].rearrange("p (u c e) -> p u e c", u=2, e=2)
 
         def update(t):
             low = tile("low%d" % t, W, F32)
@@ -159,64 +193,92 @@ def tile_picked_pqcjpxbkmin_none_p_kernel(
                         h[t][:].indirect(n1_t[:, c * W // 32 : (c + 1) * W // 32]), low[:, cols], npa[t][:, cols], ALU.add
                     )
 
-        def weigh(t):
-            nc.vector.tensor_scalar(pair_view[:, t // 2, t % 2, :], h[t][:], gs_t[:, t : t + 1], None, ALU.mult)
-
-        for t in range(3):
-            update(t)
-
         top = tile("top", PACK, F32)
-        b = []
-        for t in range(PACK):
-            acc = product("b%d" % t, t, k2_w, k2_s, x2_w, x2_s)
-            bt = tile("b%d" % t, S, F32)
-            nc.vector.tensor_scalar(bt[:], acc[:], 0.0625, None, ALU.mult, ALU.max, accum_out=top[:, t : t + 1])
-            b.append(bt)
         bias = tile("bias", PACK, F32)
-        nc.vector.scalar_tensor_tensor(bias[:], top[:], -1.0, tau_t[:], ALU.mult, ALU.mult)
+        b, b_acc, ea = {}, {}, {}
 
-        update(3)
-        for t in range(PACK):
-            weigh(t)
+        def second_layer(tiles):
+            for t in tiles:
+                acc = product("b%d" % t, t, k2_w, k2_s, x2_w, x2_s, whole)
+                b_acc[t] = acc
+                b[t] = tile("b%d" % t, S, F32)
+                nc.vector.tensor_scalar(b[t][:], acc[:], 0.0625, None, ALU.mult, ALU.max, accum_out=top[:, t : t + 1])
+                nc.vector.tensor_scalar(bias[:, t : t + 1], top[:, t : t + 1], tau_t[t][:], -1.0, ALU.mult, ALU.mult)
 
-        z = tile("z", PACK * S, BF16)
-        nc.vector.tensor_copy(
-            z[:].bitcast(I32).rearrange("p (c u) -> p c u", u=2),
-            pairs[:].bitcast(I32).rearrange("p (u c) -> p c u", u=2),
-        )
-        z_w = tile("z_w", S, U32)
-        z_s = tile("z_s", S, U8)
-        nc.vector.quantize_mx(out=z_w[:].bitcast(FP8X4), scales=z_s[:], in_=z[:])
-
-        ea = []
-        for t in range(PACK):
-            e = tile("ea%d" % t, S, F32)
+        def exponentials(t):
+            ea[t] = tile("ea%d" % t, S, F32)
             for c in range(2):
                 nc.scalar.activation(
-                    e[:, c * HALF : (c + 1) * HALF], b[t][:].indirect(n3_t[:, c * 16 : (c + 1) * 16]), ACT.Exp,
-                    bias=bias[:, t : t + 1], scale=tau_t[:, t : t + 1],
+                    ea[t][:, halves[c]], b[t][:].indirect(list_half(n3_t, c)), ACT.Exp,
+                    bias=bias[:, t : t + 1], scale=tau_t[t][:],
                 )
-            ea.append(e)
 
-        rows = out.rearrange("(p t) n -> t p n", t=PACK)
-        for t in range(PACK):
-            acc = product("h%d" % (t % 2), t, xc_w, xc_s, z_w, z_s)
-            a2 = tile("a2_%d" % t, S, F32)
-            if t == 1:
-                nc.vector.tensor_scalar(a2[:], acc[:], 0.125, None, ALU.mult)
-            else:
-                nc.scalar.activation(a2[:], acc[:], ACT.Copy, scale=0.125)
-            a4 = tile("a4_%d" % t, S, F32)
+        for t in SCALAR_SCATTER_TILES:
+            update(t)
+        xc_w, xc_s = tokens("cand", cand_t, True)
+        second_layer((0, 1))
+        update(3)
+        second_layer((2,))
+
+        planes = tile("planes", PACK * S, BF16)
+        for t in (0, 1, 3, 2):
+            nc.vector.tensor_scalar(planes[:, t * S : (t + 1) * S], h[t][:], gs_t[:, t : t + 1], None, ALU.mult)
+
+        z = tile("z", PACK * S, BF16)
+        z_w = tile("z_w", S, U32)
+        z_s = tile("z_s", S, U8)
+        by_plane = planes[:].rearrange("p (t u c i) -> p u c t i", t=PACK, u=2, i=4)
+        by_column = z[:].rearrange("p (u c i t) -> p u c t i", t=PACK, u=2, i=4)
+        for c in range(2):
+            nc.vector.tensor_copy(by_column[:, c], by_plane[:, c])
+        for c in range(2):
+            nc.vector.quantize_mx(
+                out=z_w[:, halves[c]].bitcast(FP8X4), scales=z_s[:, halves[c]],
+                in_=z[:, PACK * HALF * c : PACK * HALF * (c + 1)],
+            )
+
+        exponentials(0)
+        exponentials(1)
+        exponentials(2)
+
+        rows = out.rearrange("(g t i) n -> t g i n", t=PACK, i=RUN)
+        a2 = [tile("a2_%d" % t, S, F32) for t in range(PACK)]
+        a4 = [tile("a4_%d" % t, S, F32) for t in range(PACK)]
+        a_acc = {}
+
+        def scores(t):
+            a_acc[t] = product("h%d" % t, t, xc_w, xc_s, z_w, z_s, whole)
+            nc.vector.tensor_scalar(a2[t][:], a_acc[t][:], 0.125, None, ALU.mult)
+
+        def fetch(t):
+            for c in range(2):
+                nc.scalar.activation(a4[t][:, halves[c]], a2[t][:].indirect(list_half(n4_t, c)), ACT.Copy)
+
+        def finish(t):
             d = tile("d%d" % t, S, F32)
             m = tile("m%d" % t, S, F32)
             o = tile("o%d" % t, S, F32)
-            halves = [slice(c * HALF, (c + 1) * HALF) for c in range(2)]
-            for c in range(2):
-                nc.scalar.activation(a4[:, halves[c]], a2[:].indirect(n4_t[:, c * 16 : (c + 1) * 16]), ACT.Copy)
-            for c in halves:
-                nc.vector.tensor_tensor(d[:, c], a2[:, c], a4[:, c], ALU.subtract)
-            for c in halves:
-                nc.vector.tensor_tensor(m[:, c], d[:, c], ea[t][:, c], ALU.mult)
-            for c in halves:
-                nc.vector.scalar_tensor_tensor(o[:, c], b[t][:, c], -0.5, m[:, c], ALU.mult, ALU.add)
-            nc.sync.dma_start(rows[t], o[:])
+            last = t == PACK - 1
+            pieces = halves if last else [whole]
+            for c in pieces:
+                nc.vector.scalar_tensor_tensor(d[:, c], a_acc[t][:, c], 0.125, a4[t][:, c], ALU.mult, ALU.subtract)
+            for c in pieces:
+                (nc.vector if last else nc.gpsimd).tensor_tensor(m[:, c], d[:, c], ea[t][:, c], ALU.mult)
+            for c in pieces:
+                nc.vector.scalar_tensor_tensor(o[:, c], b_acc[t][:, c], -0.03125, m[:, c], ALU.mult, ALU.add)
+            for c in pieces:
+                nc.sync.dma_start(rows[t][:, :, c], o[:, c])
+
+        scores(0)
+        fetch(0)
+        second_layer((3,))
+        for t in (1, 2):
+            scores(t)
+            fetch(t)
+        finish(0)
+        scores(3)
+        fetch(3)
+        finish(1)
+        finish(2)
+        exponentials(3)
+        finish(3)

@@ -26,20 +26,22 @@ STAGE_AT = {
     "picked_b_k2": 768,
     "picked_w_k2": 1024,
     "words_cand": 3072,
-    "low0": 4608,
+    "old1": 4608,
     "scales_cand": 5120,
-    "low1": 6144,
     "b0": 6144,
-    "b1": 8192,
+    "old2": 7680,
+    "old3": 8192,
     "low2": 9728,
-    "b2": 10240,
-    "ea0": 12288,
-    "ra2": 13824,
-    "ea1": 14336,
-    "planes": 16384,
-    "b3": 16384,
-    "a4_2": 20480,
-    "ea3": 20480,
+    "b1": 9728,
+    "npa2": 11776,
+    "b2": 11776,
+    "ea0": 13824,
+    "ra2": 15360,
+    "ea1": 15872,
+    "planes": 17920,
+    "b3": 17920,
+    "a4_2": 22016,
+    "ea3": 22016,
 }
 
 
@@ -173,25 +175,29 @@ def tile_picked_pqcjpxbkmin_none_p_kernel(
             acc = product("h%d" % t, t, k1_w, k1_s, xq_w[1], xq_s[1], halves[0])
             nc.scalar.activation(h[t][:, halves[1]], acc[:], ACT.Copy, scale=0.0625)
             nc.scalar.activation(npa[t][:], h[t][:].indirect(n2_t[:]), ACT.Copy, scale=-0.5)
-            nc.scalar.activation(old[t][:], h[t][:].indirect(n1_t[:]), ACT.Copy)
+            if t in SCALAR_SCATTER_TILES:
+                nc.scalar.activation(old[t][:], h[t][:].indirect(n1_t[:]), ACT.Copy)
 
         k2_s = code_bytes("k2", k2_t, nc.sync)
         x2_w, x2_s = tokens("two", two_t, False)
         k2_w = code_words("k2", k2_t)
 
-        def update(t):
-            low = tile("low%d" % t, W, F32)
-            nc.vector.scalar_tensor_tensor(low[:], npa[t][:], -2.0, old[t][:], ALU.mult, ALU.min)
-            if t in SCALAR_SCATTER_TILES:
-                ra = tile("ra%d" % t, W, F32)
-                nc.vector.tensor_tensor(ra[:], low[:], npa[t][:], ALU.add)
-                nc.scalar.activation(h[t][:].indirect(n1_t[:]), ra[:], ACT.Copy)
-            else:
-                for c in range(2):
-                    cols = slice(c * W // 2, (c + 1) * W // 2)
-                    nc.vector.tensor_tensor(
-                        h[t][:].indirect(n1_t[:, c * W // 32 : (c + 1) * W // 32]), low[:, cols], npa[t][:, cols], ALU.add
-                    )
+        low = [tile("low%d" % t, W, F32) for t in range(PACK)]
+
+        def smaller(t):
+            nc.vector.scalar_tensor_tensor(low[t][:], npa[t][:], -2.0, old[t][:], ALU.mult, ALU.min)
+
+        def put_by_scalar(t):
+            ra = tile("ra%d" % t, W, F32)
+            nc.gpsimd.tensor_tensor(ra[:], low[t][:], npa[t][:], ALU.add)
+            nc.scalar.activation(h[t][:].indirect(n1_t[:]), ra[:], ACT.Copy)
+
+        def put_by_vector(t):
+            for c in range(2):
+                cols = slice(c * W // 2, (c + 1) * W // 2)
+                nc.vector.tensor_tensor(
+                    h[t][:].indirect(n1_t[:, c * W // 32 : (c + 1) * W // 32]), low[t][:, cols], npa[t][:, cols], ALU.add
+                )
 
         top = tile("top", PACK, F32)
         bias = tile("bias", PACK, F32)
@@ -214,14 +220,19 @@ def tile_picked_pqcjpxbkmin_none_p_kernel(
                 )
 
         for t in SCALAR_SCATTER_TILES:
-            update(t)
+            smaller(t)
+            put_by_scalar(t)
         xc_w, xc_s = tokens("cand", cand_t, True)
+        nc.vector.tensor_copy(old[3][:], h[3][:].indirect(n1_t[:]))
+        smaller(3)
         second_layer((0, 1))
-        update(3)
+        put_by_vector(3)
         second_layer((2,))
 
         planes = tile("planes", PACK * S, BF16)
-        for t in (0, 1, 3, 2):
+        for t in (0, 1):
+            nc.gpsimd.tensor_scalar(planes[:, t * S : (t + 1) * S], h[t][:], gs_t[:, t : t + 1], 0.0, ALU.mult, ALU.add)
+        for t in (3, 2):
             nc.vector.tensor_scalar(planes[:, t * S : (t + 1) * S], h[t][:], gs_t[:, t : t + 1], None, ALU.mult)
 
         z = tile("z", PACK * S, BF16)

@@ -20,28 +20,34 @@ PACK = 4
 HALF = S // 2
 RUN = 4
 SCALAR_SCATTER_TILES = (0, 1, 2)
+SCALAR_OLD_TILES = (0, 1)
 STAGE_AT = {
-    "words_offs0": 0,
-    "scales_two": 0,
-    "picked_b_k2": 768,
-    "picked_w_k2": 1024,
-    "words_cand": 3072,
-    "old1": 4608,
-    "scales_cand": 5120,
-    "b0": 6144,
-    "old2": 7680,
-    "old3": 8192,
-    "low2": 9728,
-    "b1": 9728,
-    "npa2": 11776,
-    "b2": 11776,
-    "ea0": 13824,
-    "ra2": 15360,
-    "ea1": 15872,
-    "planes": 17920,
-    "b3": 17920,
-    "a4_2": 22016,
-    "ea3": 22016,
+    "words_two": 0,
+    "picked_w_k1": 1984,
+    "scales_two": 2048,
+    "picked_b_k2": 3776,
+    "picked_w_k2": 4032,
+    "scales_offs": 6144,
+    "picked_b_k1": 6400,
+    "words_offs": 6656,
+    "words_cand": 8704,
+    "old1": 10240,
+    "scales_cand": 10752,
+    "old2": 11264,
+    "b0": 11264,
+    "low1": 13312,
+    "old3": 13312,
+    "low2": 14848,
+    "b1": 14848,
+    "npa2": 16896,
+    "b2": 16896,
+    "ea0": 18944,
+    "ra2": 20480,
+    "ea1": 20992,
+    "planes": 23040,
+    "b3": 23040,
+    "a4_2": 27136,
+    "ea3": 27136,
 }
 
 
@@ -80,12 +86,12 @@ def tile_picked_pqcjpxbkmin_none_p_kernel(
         offs_t = load_list("offs_t", offs)
         k2_t = load_list("k2_t", k2)
         two_t = load_list("two_t", two)
-        d_tab = tile("d_tab", G, U32)
-        nc.sync.dma_start(d_tab[:].bitcast(I32), d_words[0].rearrange("p n t -> p (n t)").bitcast(I32))
-        for q in range(4):
-            nc.sync.dma_start(x_bytes[32 * q : 32 * q + 4, :].bitcast(I32), x_scales[0, 4 * q : 4 * q + 4, :].bitcast(I32))
         x_tab = tile("x_tab", T, U32)
         nc.sync.dma_start(x_tab[:].bitcast(I32), x_words[0].rearrange("p n t -> p (n t)").bitcast(I32))
+        for q in range(4):
+            nc.sync.dma_start(x_bytes[32 * q : 32 * q + 4, :].bitcast(I32), x_scales[0, 4 * q : 4 * q + 4, :].bitcast(I32))
+        d_tab = tile("d_tab", G, U32)
+        nc.sync.dma_start(d_tab[:].bitcast(I32), d_words[0].rearrange("p n t -> p (n t)").bitcast(I32))
         n2_t = load_list("n2_t", n2)
         n1_t = load_list("n1_t", n1)
         cand_t = load_list("cand_t", cand)
@@ -159,23 +165,16 @@ def tile_picked_pqcjpxbkmin_none_p_kernel(
             return acc
 
         k1_s = code_bytes("k1", k1_t, nc.scalar)
+        xq_w, xq_s = tokens("offs", offs_t, False)
         k1_w = code_words("k1", k1_t)
-        xq_w = [tile("words_offs%d" % c, HALF, U32) for c in range(2)]
-        xq_s = [tile("scales_offs%d" % c, HALF, U8) for c in range(2)]
-        for c in range(2):
-            nc.vector.tensor_copy(xq_s[c][:], x_bytes[:].indirect(list_half(offs_t, c)))
-            nc.vector.tensor_copy(xq_w[c][:], x_tab[:].indirect(list_half(offs_t, c)))
         h = [tile("h%d" % t, S, F32) for t in range(PACK)]
         npa = [tile("npa%d" % t, W, F32) for t in range(PACK)]
         old = [tile("old%d" % t, W, F32) for t in range(PACK)]
         for t in range(PACK):
-            acc = product("b%d" % t, t, k1_w, k1_s, xq_w[0], xq_s[0], halves[0])
-            nc.scalar.activation(h[t][:, halves[0]], acc[:], ACT.Copy, scale=0.0625)
-        for t in range(PACK):
-            acc = product("h%d" % t, t, k1_w, k1_s, xq_w[1], xq_s[1], halves[0])
-            nc.scalar.activation(h[t][:, halves[1]], acc[:], ACT.Copy, scale=0.0625)
+            acc = product("h%d" % t, t, k1_w, k1_s, xq_w, xq_s, whole)
+            nc.scalar.activation(h[t][:], acc[:], ACT.Copy, scale=0.0625)
             nc.scalar.activation(npa[t][:], h[t][:].indirect(n2_t[:]), ACT.Copy, scale=-0.5)
-            if t in SCALAR_SCATTER_TILES:
+            if t in SCALAR_OLD_TILES:
                 nc.scalar.activation(old[t][:], h[t][:].indirect(n1_t[:]), ACT.Copy)
 
         k2_s = code_bytes("k2", k2_t, nc.sync)
@@ -185,6 +184,8 @@ def tile_picked_pqcjpxbkmin_none_p_kernel(
         low = [tile("low%d" % t, W, F32) for t in range(PACK)]
 
         def smaller(t):
+            if t not in SCALAR_OLD_TILES:
+                nc.vector.tensor_copy(old[t][:], h[t][:].indirect(n1_t[:]))
             nc.vector.scalar_tensor_tensor(low[t][:], npa[t][:], -2.0, old[t][:], ALU.mult, ALU.min)
 
         def put_by_scalar(t):
@@ -223,16 +224,15 @@ def tile_picked_pqcjpxbkmin_none_p_kernel(
             smaller(t)
             put_by_scalar(t)
         xc_w, xc_s = tokens("cand", cand_t, True)
-        nc.vector.tensor_copy(old[3][:], h[3][:].indirect(n1_t[:]))
         smaller(3)
         second_layer((0, 1))
         put_by_vector(3)
         second_layer((2,))
 
         planes = tile("planes", PACK * S, BF16)
-        for t in (0, 1):
+        for t in SCALAR_SCATTER_TILES:
             nc.gpsimd.tensor_scalar(planes[:, t * S : (t + 1) * S], h[t][:], gs_t[:, t : t + 1], 0.0, ALU.mult, ALU.add)
-        for t in (3, 2):
+        for t in (3,):
             nc.vector.tensor_scalar(planes[:, t * S : (t + 1) * S], h[t][:], gs_t[:, t : t + 1], None, ALU.mult)
 
         z = tile("z", PACK * S, BF16)

from contextlib import ExitStack

import concourse.mybir as mybir

K, T, S, G, H, W, C = 512, 1024, 512, 2048, 512, 384, 512
FLOPS = 3 * 2 * 512 * 512 * 512

F32 = mybir.dt.float32
BF16 = mybir.dt.bfloat16
I32 = mybir.dt.int32
U32 = mybir.dt.uint32
U16 = mybir.dt.uint16
U8 = mybir.dt.uint8
FP8X4 = mybir.dt.float8_e4m3fn_x4
ALU = mybir.AluOpType
ACT = mybir.ActivationFunctionType

P = 128
PACK = 4
HALF = S // 2
RUN = 4
SCALAR_SCATTER_TILES = (0, 1, 2)
SCALAR_OLD_TILES = (0, 1)
STAGE_AT = {
    "words_two": 0,
    "picked_w_k1": 1984,
    "scales_two": 2048,
    "picked_b_k2": 3776,
    "picked_w_k2": 4032,
    "scales_offs": 6144,
    "picked_b_k1": 6400,
    "words_offs": 6656,
    "words_cand": 8704,
    "old1": 10240,
    "scales_cand": 10752,
    "old2": 11264,
    "b0": 11264,
    "low1": 13312,
    "old3": 13312,
    "low2": 14848,
    "b1": 14848,
    "npa2": 16896,
    "b2": 16896,
    "ea0": 18944,
    "ra2": 20480,
    "ea1": 20992,
    "planes": 23040,
    "b3": 23040,
    "a4_2": 27136,
    "ea3": 27136,
}


def tile_picked_pqcjpxbkmin_none_p_kernel(
    tc, x_words, x_scales, d_words, d_scales, gs, tau, offs, k1, n1, n2, cand, two, k2, n3, n4, out
):
    nc = tc.nc
    with ExitStack() as ctx:
        keep = ctx.enter_context(tc.tile_pool(name="keep", bufs=1))
        psum = ctx.enter_context(tc.psum_pool(name="psum", bufs=1))

        stage = ctx.enter_context(tc.tile_pool(name="stage", bufs=1))

        def tile(name, width, dtype):
            if name in STAGE_AT:
                return stage.tile([P, width], dtype, name=name, align_bytes=64, offset=STAGE_AT[name])
            return keep.tile([P, width], dtype, name=name, align_bytes=64)

        def load_list(name, src):
            t = keep.tile([P, src.shape[1]], U16, name=name)
            nc.sync.dma_start(t[:], src)
            return t

        def zeroed_bytes(name, width, engine):
            t = tile(name, width, U8)
            engine.memset(t[:].bitcast(I32), 0)
            return t

        d_bytes = zeroed_bytes("d_bytes", G, nc.vector)
        x_bytes = zeroed_bytes("x_bytes", T, nc.vector)

        d_rows = d_scales[0].rearrange("(r e) n -> e r n", e=2)
        for e in range(2):
            nc.sync.dma_start(d_bytes[e:P:16, :].bitcast(I32), d_rows[e].bitcast(I32))
        k1_t = load_list("k1_t", k1)
        offs_t = load_list("offs_t", offs)
        k2_t = load_list("k2_t", k2)
        two_t = load_list("two_t", two)
        x_tab = tile("x_tab", T, U32)
        nc.sync.dma_start(x_tab[:].bitcast(I32), x_words[0].rearrange("p n t -> p (n t)").bitcast(I32))
        for q in range(4):
            nc.sync.dma_start(x_bytes[32 * q : 32 * q + 4, :].bitcast(I32), x_scales[0, 4 * q : 4 * q + 4, :].bitcast(I32))
        d_tab = tile("d_tab", G, U32)
        nc.sync.dma_start(d_tab[:].bitcast(I32), d_words[0].rearrange("p n t -> p (n t)").bitcast(I32))
        n2_t = load_list("n2_t", n2)
        n1_t = load_list("n1_t", n1)
        cand_t = load_list("cand_t", cand)
        gs_t = tile("gs_t", PACK, F32)
        nc.sync.dma_start(gs_t[:], gs.rearrange("(p t) o -> p (t o)", t=PACK))
        tau_rows = tau.rearrange("(g t i) o -> t g i o", t=PACK, i=RUN)
        tau_t = [tile("tau%d" % t, 1, F32) for t in range(PACK)]
        n3_t = load_list("n3_t", n3)
        for t in range(PACK):
            with nc.allow_non_contiguous_dma(reason="one rate for each partition"):
                nc.sync.dma_start(tau_t[t][:], tau_rows[t])
        n4_t = load_list("n4_t", n4)

        def code_bytes(name, lst, queue):
            picked = tile("picked_b_" + name, H, U8)
            nc.vector.tensor_copy(picked[:], d_bytes[:].indirect(lst[:]))
            dealt = tile("dealt_b_" + name, H, U8)
            placed = tile("placed_" + name, H, U8)
            if name == "k1":
                nc.vector.tensor_copy(
                    dealt[:].rearrange("p (t m) -> p t m", t=PACK), picked[:].rearrange("p (m t) -> p t m", t=PACK)
                )
                nc.vector.tensor_copy(placed[:].bitcast(I32), dealt[:].bitcast(I32))
            else:
                for dst in (dealt, placed):
                    nc.vector.tensor_copy(
                        dst[:].bitcast(I32).rearrange("p (t g) -> p t g", t=PACK),
                        picked[:].bitcast(I32).rearrange("p (g t) -> p t g", t=PACK),
                    )
            for e in range(2):
                queue.dma_start(placed[2 + e : P : 32, :].bitcast(I32), dealt[16 + e : P : 32, :].bitcast(I32))
            return placed

        def code_words(name, lst):
            picked = tile("picked_w_" + name, H, U32)
            nc.vector.tensor_copy(picked[:], d_tab[:].indirect(lst[:]))
            dealt = tile("dealt_w_" + name, H, U32)
            if name == "k1":
                nc.vector.tensor_copy(
                    dealt[:].rearrange("p (t m i) -> p m t i", t=PACK, i=4),
                    picked[:].rearrange("p (m i t) -> p m t i", t=PACK, i=4),
                )
            else:
                nc.vector.tensor_copy(
                    dealt[:].rearrange("p (t g i) -> p t g i", t=PACK, i=RUN),
                    picked[:].rearrange("p (g t i) -> p t g i", t=PACK, i=RUN),
                )
            return dealt

        def tokens(name, lst, dealt):
            words = tile("words_" + name, S, U32)
            scales = tile("scales_" + name, S, U8)
            for dst, table in ((words, x_tab), (scales, x_bytes)):
                view = dst[:].rearrange("p (t g i) -> p g t i", t=PACK, i=RUN) if dealt else dst[:]
                nc.vector.tensor_copy(view, table[:].indirect(lst[:]))
            return words, scales

        halves = [slice(c * HALF, (c + 1) * HALF) for c in range(2)]
        whole = slice(0, S)

        def list_half(lst, c):
            return lst[:, c * HALF // 16 : (c + 1) * HALF // 16]

        def product(bank, t, lhs_w, lhs_s, rhs_w, rhs_s, cols):
            acc = psum.tile([P, cols.stop - cols.start], F32, name="acc", tag=bank)
            rows_t = slice(P * t, P * (t + 1))
            nc.tensor.matmul_mx(
                out=acc[:], lhsT=lhs_w[:, rows_t].bitcast(FP8X4), lhsT_scale=lhs_s[:, rows_t],
                rhs=rhs_w[:, cols].bitcast(FP8X4), rhs_scale=rhs_s[:, cols], start=True, stop=True,
            )
            return acc

        k1_s = code_bytes("k1", k1_t, nc.scalar)
        xq_w, xq_s = tokens("offs", offs_t, False)
        k1_w = code_words("k1", k1_t)
        h = [tile("h%d" % t, S, F32) for t in range(PACK)]
        npa = [tile("npa%d" % t, W, F32) for t in range(PACK)]
        old = [tile("old%d" % t, W, F32) for t in range(PACK)]
        for t in range(PACK):
            acc = product("h%d" % t, t, k1_w, k1_s, xq_w, xq_s, whole)
            nc.scalar.activation(h[t][:], acc[:], ACT.Copy, scale=0.0625)
            nc.scalar.activation(npa[t][:], h[t][:].indirect(n2_t[:]), ACT.Copy, scale=-0.5)
            if t in SCALAR_OLD_TILES:
                nc.scalar.activation(old[t][:], h[t][:].indirect(n1_t[:]), ACT.Copy)

        k2_s = code_bytes("k2", k2_t, nc.sync)
        x2_w, x2_s = tokens("two", two_t, False)
        k2_w = code_words("k2", k2_t)

        low = [tile("low%d" % t, W, F32) for t in range(PACK)]

        def smaller(t):
            if t not in SCALAR_OLD_TILES:
                nc.vector.tensor_copy(old[t][:], h[t][:].indirect(n1_t[:]))
            nc.vector.scalar_tensor_tensor(low[t][:], npa[t][:], -2.0, old[t][:], ALU.mult, ALU.min)

        def put_by_scalar(t):
            ra = tile("ra%d" % t, W, F32)
            nc.gpsimd.tensor_tensor(ra[:], low[t][:], npa[t][:], ALU.add)
            nc.scalar.activation(h[t][:].indirect(n1_t[:]), ra[:], ACT.Copy)

        def put_by_vector(t):
            for c in range(2):
                cols = slice(c * W // 2, (c + 1) * W // 2)
                nc.vector.tensor_tensor(
                    h[t][:].indirect(n1_t[:, c * W // 32 : (c + 1) * W // 32]), low[t][:, cols], npa[t][:, cols], ALU.add
                )

        top = tile("top", PACK, F32)
        bias = tile("bias", PACK, F32)
        b, b_acc, ea = {}, {}, {}

        def second_layer(tiles):
            for t in tiles:
                acc = product("b%d" % t, t, k2_w, k2_s, x2_w, x2_s, whole)
                b_acc[t] = acc
                b[t] = tile("b%d" % t, S, F32)
                nc.vector.tensor_scalar(b[t][:], acc[:], 0.0625, None, ALU.mult, ALU.max, accum_out=top[:, t : t + 1])
                nc.vector.tensor_scalar(bias[:, t : t + 1], top[:, t : t + 1], tau_t[t][:], -1.0, ALU.mult, ALU.mult)

        def exponentials(t):
            ea[t] = tile("ea%d" % t, S, F32)
            for c in range(2):
                nc.scalar.activation(
                    ea[t][:, halves[c]], b[t][:].indirect(list_half(n3_t, c)), ACT.Exp,
                    bias=bias[:, t : t + 1], scale=tau_t[t][:],
                )

        for t in SCALAR_SCATTER_TILES:
            smaller(t)
            put_by_scalar(t)
        xc_w, xc_s = tokens("cand", cand_t, True)
        smaller(3)
        second_layer((0, 1))
        put_by_vector(3)
        second_layer((2,))

        planes = tile("planes", PACK * S, BF16)
        for t in SCALAR_SCATTER_TILES:
            nc.gpsimd.tensor_scalar(planes[:, t * S : (t + 1) * S], h[t][:], gs_t[:, t : t + 1], 0.0, ALU.mult, ALU.add)
        for t in (3,):
            nc.vector.tensor_scalar(planes[:, t * S : (t + 1) * S], h[t][:], gs_t[:, t : t + 1], None, ALU.mult)

        z = tile("z", PACK * S, BF16)
        z_w = tile("z_w", S, U32)
        z_s = tile("z_s", S, U8)
        by_plane = planes[:].rearrange("p (t u c i) -> p u c t i", t=PACK, u=2, i=4)
        by_column = z[:].rearrange("p (u c i t) -> p u c t i", t=PACK, u=2, i=4)
        for c in range(2):
            nc.vector.tensor_copy(by_column[:, c], by_plane[:, c])
        for c in range(2):
            nc.vector.quantize_mx(
                out=z_w[:, halves[c]].bitcast(FP8X4), scales=z_s[:, halves[c]],
                in_=z[:, PACK * HALF * c : PACK * HALF * (c + 1)],
            )

        exponentials(0)
        exponentials(1)
        exponentials(2)

        rows = out.rearrange("(g t i) n -> t g i n", t=PACK, i=RUN)
        a2 = [tile("a2_%d" % t, S, F32) for t in range(PACK)]
        a4 = [tile("a4_%d" % t, S, F32) for t in range(PACK)]
        a_acc = {}

        def scores(t):
            a_acc[t] = product("h%d" % t, t, xc_w, xc_s, z_w, z_s, whole)
            nc.vector.tensor_scalar(a2[t][:], a_acc[t][:], 0.125, None, ALU.mult)

        def fetch(t):
            for c in range(2):
                nc.scalar.activation(a4[t][:, halves[c]], a2[t][:].indirect(list_half(n4_t, c)), ACT.Copy)

        def finish(t):
            d = tile("d%d" % t, S, F32)
            m = tile("m%d" % t, S, F32)
            o = tile("o%d" % t, S, F32)
            last = t == PACK - 1
            pieces = halves if last else [whole]
            for c in pieces:
                nc.vector.scalar_tensor_tensor(d[:, c], a_acc[t][:, c], 0.125, a4[t][:, c], ALU.mult, ALU.subtract)
            for c in pieces:
                (nc.vector if last else nc.gpsimd).tensor_tensor(m[:, c], d[:, c], ea[t][:, c], ALU.mult)
            for c in pieces:
                nc.vector.scalar_tensor_tensor(o[:, c], b_acc[t][:, c], -0.03125, m[:, c], ALU.mult, ALU.add)
            for c in pieces:
                nc.sync.dma_start(rows[t][:, :, c], o[:, c])

        scores(0)
        fetch(0)
        second_layer((3,))
        for t in (1, 2):
            scores(t)
            fetch(t)
        finish(0)
        scores(3)
        fetch(3)
        finish(1)
        finish(2)
        exponentials(3)
        finish(3)
